import numpy as np
import ml_dtypes


def mxq(x, axis, fmt="e4m3"):
    dtype, down = {"e4m3": (ml_dtypes.float8_e4m3fn, 7), "e5m2": (ml_dtypes.float8_e5m2, 14)}[fmt]
    v = np.moveaxis(np.asarray(x, np.float32).astype(ml_dtypes.bfloat16).astype(np.float64), axis, -1)
    blocks = v.reshape(v.shape[:-1] + (-1, 32))
    amax = np.abs(blocks).max(-1, keepdims=True)
    byte = np.maximum(np.where(amax > 0, np.frexp(amax)[1] - 1 + 127, 0) - down, 1)
    scale = np.exp2(byte - 127.0)
    codes = (blocks / scale).astype(np.float32).astype(dtype).astype(np.float64)
    return np.moveaxis((codes * scale).reshape(v.shape), -1, axis)


WIDE = False


def mx_kscale(k):
    if not WIDE:
        return np.ones(k)
    levels = np.array([10, -10, 5, -5, 0])
    if k % 512:
        return np.exp2(np.random.permutation(np.resize(levels, k // 32))).repeat(32)
    a = np.empty((k // 512, 16))
    for p in range(k // 512):
        a[p, :8] = np.random.permutation(np.resize(levels, 8))
        for g in range(8):
            far = levels[np.abs(levels - a[p, g]) >= 10]
            a[p, g + 8] = far[np.random.randint(len(far))]
    return np.exp2(a.ravel()).repeat(32)


def f64(x):
    return np.asarray(x).astype(np.float64)


def striped(idx):
    return np.tile(idx.reshape(-1, 16).T, (8, 1)).astype(np.uint16)


def unstriped(offs):
    return offs[:16].T.reshape(-1).astype(np.int64)


def pack_weight(w):
    k, n = w.shape
    w = f64(np.asarray(w, np.float32).astype(ml_dtypes.bfloat16)).reshape(k // 32, 32, n)
    amax = np.abs(w).max(1)
    byte = np.clip(np.where(amax > 0, np.frexp(amax)[1] - 1 + 127 - 7, 1), 1, 254)
    scaled = (w * np.exp2(127.0 - byte)[:, None, :]).reshape(k, n).astype(np.float32)
    words = np.ascontiguousarray(scaled.reshape(k // 512, 128, 4, n).transpose(0, 1, 3, 2)).astype(ml_dtypes.float8_e4m3fn).view(np.uint8)
    return words, np.ascontiguousarray(byte.astype(np.uint8).reshape(k // 512, 16, n))


def unpack_weight(words, scales):
    g, p, n, _ = words.shape
    vals = np.ascontiguousarray(words).view(ml_dtypes.float8_e4m3fn).astype(np.float64) * np.repeat(np.exp2(scales.astype(np.float64) - 127.0), 8, axis=1)[..., None]
    return vals.transpose(0, 1, 3, 2).reshape(g * 512, n)


E2M1 = np.array([0.0, 0.5, 1.0, 1.5, 2.0, 3.0, 4.0, 6.0, -0.0, -0.5, -1.0, -1.5, -2.0, -3.0, -4.0, -6.0])


def pack_fp4(w):
    k, n = w.shape
    w = f64(np.asarray(w, np.float32).astype(ml_dtypes.bfloat16)).reshape(k // 32, 32, n)
    amax = np.abs(w).max(1)
    mant, ex = np.frexp(amax / 6.0)
    byte = np.clip(np.where(amax > 0, np.where(mant > 0.5, ex, ex - 1) + 127, 1), 1, 254)
    scaled = (w * np.exp2(127.0 - byte)[:, None, :]).reshape(k, n).astype(np.float32)
    c = np.ascontiguousarray(scaled.reshape(k // 512, 128, 4, n).transpose(0, 1, 3, 2)).astype(ml_dtypes.float4_e2m1fn).view(np.uint8) & 0xF
    words = (c[..., 0::2] | (c[..., 1::2] << 4)).reshape(k // 512, 128, 2 * n)
    return np.ascontiguousarray(words), np.ascontiguousarray(byte.astype(np.uint8).reshape(k // 512, 16, n))


def unpack_fp4(words, scales):
    g, _, n = scales.shape
    words = np.ascontiguousarray(words).reshape(g, 128, n, 2)
    nib = np.empty((g, 128, n, 4), np.uint8)
    nib[..., 0::2] = words & 0xF
    nib[..., 1::2] = words >> 4
    vals = E2M1[nib] * np.repeat(np.exp2(scales.astype(np.float64) - 127.0), 8, axis=1)[..., None]
    return vals.transpose(0, 1, 3, 2).reshape(g * 512, n)


def planes(y):
    n, m = y.shape
    v = y.astype(np.float32).astype(ml_dtypes.bfloat16).astype(np.float64).reshape(n // 32, 32, m)
    top = np.abs(v).max(1)
    byte = np.clip(np.where(top > 0, np.frexp(top)[1] - 1 + 127 - 7, 1), 1, 254)
    codes = (v * np.exp2(127.0 - byte)[:, None, :]).reshape(n, m).astype(np.float32).astype(ml_dtypes.float8_e4m3fn).view(np.uint8)
    words = codes.reshape(n // 512, 128, 4, m).transpose(0, 1, 3, 2)
    return np.ascontiguousarray(words), np.ascontiguousarray(byte.astype(np.uint8).reshape(n // 512, 16, m))


K, T, S, H, Z, W = 512, 2048, 512, 512, 512, 1024
P = 2 ** 7


def setup_inputs():
    n = np.random.standard_normal
    s = mx_kscale(K)[:, None]
    u = mx_kscale(H)
    packed_xT = pack_weight(n((K, T)) * s)
    packed_w1 = pack_fp4(n((K, H)) / np.sqrt(K) / s)
    packed_w2 = pack_fp4(n((K, H)) / np.sqrt(K) / s)
    packed_eT = pack_weight(n((K, W)) * s)
    packed_w3 = pack_fp4(n((K, H)) / np.sqrt(K) / s)
    return {
        "x_words": packed_xT[0],
        "x_scales": packed_xT[1],
        "w1_words": packed_w1[0],
        "w1_scales": packed_w1[1],
        "w2_words": packed_w2[0],
        "w2_scales": packed_w2[1],
        "e_words": packed_eT[0],
        "e_scales": packed_eT[1],
        "w3_words": packed_w3[0],
        "w3_scales": packed_w3[1],
        "unit": (np.random.uniform(0.6, 1.4, (H, 1)) * u[:, None]).astype(np.float32),
        "unit2": (np.random.uniform(0.6, 1.4, (H, 1)) / np.sqrt(H) / u[:, None]).astype(np.float32),
        "vol": (np.tile(np.random.uniform(0.4, 1.5, W), (P, 1))).astype(np.float32),
        "offs": striped(np.random.permutation(T)[:S]),
        "hdg": striped(np.random.permutation(W)[:Z]),
        "sec": striped(np.random.permutation(S)),
        "prx": striped(np.random.permutation(Z)),
    }


def reference(x_words, x_scales, w1_words, w1_scales, w2_words, w2_scales, e_words, e_scales, w3_words, w3_scales, unit, unit2, vol, offs, hdg, sec, prx):
    xq = unpack_weight(x_words, x_scales)[:, unstriped(offs)]
    y = unpack_fp4(w1_words, w1_scales).T @ xq
    yv = unpack_fp4(w2_words, w2_scales).T @ xq
    vs = yv[:, unstriped(sec)]
    load = y + 0.5 * vs
    hid = f64(unit) * load
    e_hdg = unpack_weight(e_words, e_scales)[:, unstriped(hdg)]
    ye = unpack_fp4(w3_words, w3_scales).T @ e_hdg
    hid2 = f64(unit2) * ye
    sc = mxq(hid, 0, "e4m3").T @ mxq(hid2, 0, "e4m3")
    beta_ = sc / (f64(vol)[:1][:, unstriped(hdg)])
    bp = beta_[:, unstriped(prx)]
    b2 = (beta_) ** 2
    expl = b2.mean(axis=1, keepdims=True)
    out_0 = beta_ * bp - expl
    return (out_0,) + planes(out_0)

@@ -1,0 +1,291 @@
+from contextlib import ExitStack
+
+import concourse.mybir as mybir
+from concourse.masks import make_identity
+
+K, T, S, H, Z, W = 512, 2048, 512, 512, 512, 1024
+FLOPS = 4 * 2 * 512 * 512 * 512
+
+F32 = mybir.dt.float32
+BF16 = mybir.dt.bfloat16
+I32 = mybir.dt.int32
+U32 = mybir.dt.uint32
+U16 = mybir.dt.uint16
+U8 = mybir.dt.uint8
+FP8X4 = mybir.dt.float8_e4m3fn_x4
+FP4X4 = mybir.dt.float4_e2m1fn_x4
+ALU = mybir.AluOpType
+ACT = mybir.ActivationFunctionType
+
+P = 128
+PACK = 4
+QUAD = 32
+HALF = 256
+SPLIT = 320
+
+
+def tile_picked_yfcovr_cross_po_kernel(
+    tc, x_words, x_scales, w1_words, w1_scales, w2_words, w2_scales, e_words, e_scales, w3_words, w3_scales,
+    unit, unit2, vol, offs, hdg, sec, prx, out_0, out_1, out_2,
+):
+    nc = tc.nc
+    with ExitStack() as ctx:
+        sb = ctx.enter_context(tc.tile_pool(name="sb", bufs=1))
+        ps = ctx.enter_context(tc.psum_pool(name="ps", bufs=1))
+
+        def tile(name, shape, dtype):
+            return sb.tile(shape, dtype, name=name, align_bytes=64)
+
+        def bank(b, name, shape):
+            return ps.tile(shape, F32, name=name, tag="bank%d" % b)
+
+        def load_list(name, src):
+            t = sb.tile([P, 32], U16, name=name)
+            nc.sync.dma_start(t[:], src)
+            return t
+
+        def cleared(name, cols):
+            t = tile(name, [P, cols], U8)
+            nc.vector.memset(t[:].bitcast(I32), 0)
+            return t
+
+        def load_scale_rows(dst, src, queues):
+            for q in range(4):
+                queues[q].dma_start(dst[QUAD * q : QUAD * q + 4, :].bitcast(I32), src[0, 4 * q : 4 * q + 4, :].bitcast(I32))
+
+        def load_words(name, src, cols):
+            t = tile(name, [P, cols], U32)
+            nc.sync.dma_start(t[:].bitcast(I32), src[0].rearrange("p c r -> p (c r)").bitcast(I32))
+            return t
+
+        def load_fp4(name, src):
+            t = tile(name, [P, 2 * H], U8)
+            nc.sync.dma_start(t[:].bitcast(I32), src[0].bitcast(I32))
+            return t
+
+        def deal_fp4(name, raw):
+            t = tile(name, [P, 2 * H], U8)
+            nc.vector.tensor_copy(
+                t[:].bitcast(I32).rearrange("p (t g c) -> p t g c", t=PACK, c=4),
+                raw[:].bitcast(I32).rearrange("p (g t c) -> p t g c", t=PACK, c=4),
+            )
+            return t
+
+        def deal_scales(name, raw):
+            t = tile(name, [P, H], U8)
+            nc.vector.tensor_copy(
+                t[:].bitcast(I32).rearrange("p (t g c) -> p t g c", t=PACK, c=2),
+                raw.bitcast(I32).rearrange("p (g t c) -> p t g c", t=PACK, c=2),
+            )
+            return t
+
+        def halves(offsets):
+            return [(slice(h * HALF, (h + 1) * HALF), offsets[:, 16 * h : 16 * (h + 1)]) for h in range(2)]
+
+        xs_all = cleared("xs_all", T)
+        rows = tile("rows", [P, P], F32)
+        nc.vector.memset(rows[:], 0.0)
+        ws_raw = cleared("ws_raw", 3 * H)
+        ws1_raw, ws2_raw, ws3_raw = (ws_raw[:, i * H : (i + 1) * H] for i in range(3))
+        es_all = cleared("es_all", W)
+        for i, src in enumerate((unit, unit2)):
+            nc.gpsimd.dma_start(
+                rows[4 * i : 4 * i + 4, :].rearrange("t (g r) -> t g r", r=8),
+                src.rearrange("(g t r) o -> t g (r o)", t=PACK, r=8),
+            )
+        ident = tile("ident", [P, P], F32)
+        make_identity(nc, ident[:])
+        load_scale_rows(ws1_raw, w1_scales, (nc.gpsimd,) * 4)
+
+        offs_t = load_list("offs_t", offs)
+        vol_col = tile("vol_col", [P, 8], F32)
+        nc.scalar.dma_start(vol_col[:], vol[0].rearrange("(p c) -> p c", c=8))
+        load_scale_rows(xs_all[:], x_scales, (nc.sync, nc.sync, nc.scalar, nc.scalar))
+        xw_all = load_words("xw_all", x_words, T)
+        w2_raw = load_fp4("w2_raw", w2_words)
+        load_scale_rows(ws2_raw, w2_scales, (nc.scalar, nc.scalar, nc.scalar, nc.sync))
+        hdg_t = load_list("hdg_t", hdg)
+        ew_all = load_words("ew_all", e_words, W)
+        load_scale_rows(es_all[:], e_scales, (nc.sync,) * 4)
+        sec_t = load_list("sec_t", sec)
+        load_scale_rows(ws3_raw, w3_scales, (nc.sync,) * 4)
+        w3_raw = load_fp4("w3_raw", w3_words)
+        w1_raw = load_fp4("w1_raw", w1_words)
+        prx_t = load_list("prx_t", prx)
+
+        inv_col = tile("inv_col", [P, 8], F32)
+        nc.vector.reciprocal(inv_col[:], vol_col[:])
+        xs = tile("xs", [P, S], U8)
+        nc.vector.tensor_copy(xs[:], xs_all[:].indirect(offs_t[:]))
+
+        inv_all = tile("inv_all", [P, P, 8], F32)
+        for b in range(2):
+            spread = bank(5 + b, "spread%d" % b, [P, 4, P])
+            for c in range(4):
+                col = 4 * b + c
+                nc.tensor.transpose(spread[:, c, :], inv_col[:, col : col + 1].to_broadcast([P, P]), ident[:])
+            nc.scalar.activation(inv_all[:, :, 4 * b : 4 * b + 4], spread[:].rearrange("p c n -> p n c"), ACT.Copy)
+        turned = bank(7, "turned", [P, P])
+        nc.tensor.transpose(turned[:], rows[:], ident[:])
+        units = tile("units", [P, 8], F32)
+        half_unit = tile("half_unit", [P, PACK], F32)
+        nc.scalar.activation(half_unit[:], turned[:, 0:4], ACT.Copy, scale=0.5)
+        nc.scalar.activation(units[:], turned[:, 0:8], ACT.Copy)
+        inv_vol = tile("inv_vol", [P, Z], F32)
+        nc.scalar.activation(inv_vol[:], inv_all[:].rearrange("p n c -> p (n c)").indirect(hdg_t[:]), ACT.Copy)
+
+        xw = tile("xw", [P, S], U32)
+        nc.vector.tensor_copy(xw[:], xw_all[:].indirect(offs_t[:]))
+        ws2 = deal_scales("ws2", ws2_raw)
+        w2 = deal_fp4("w2", w2_raw)
+
+        def product(out, w, w_scales, t, words, scales):
+            nc.tensor.matmul_mx(
+                out,
+                lhsT=w[:, 2 * P * t : 2 * P * (t + 1)].bitcast(FP4X4),
+                lhsT_scale=w_scales[:, P * t : P * (t + 1)],
+                rhs=words.bitcast(FP8X4),
+                rhs_scale=scales,
+                start=True,
+                stop=True,
+            )
+
+        yv_ps = [bank(t, "yv%d" % t, [P, S]) for t in range(PACK)]
+        for t in range(PACK):
+            product(yv_ps[t][:], w2, ws2, t, xw[:], xs[:])
+
+        ew = tile("ew", [P, Z], U32)
+        nc.vector.tensor_copy(ew[:], ew_all[:].indirect(hdg_t[:]))
+        es = tile("es", [P, Z], U8)
+        nc.vector.tensor_copy(es[:], es_all[:].indirect(hdg_t[:]))
+        ws3 = deal_scales("ws3", ws3_raw)
+        w3 = deal_fp4("w3", w3_raw)
+        ws1 = deal_scales("ws1", ws1_raw)
+        w1 = deal_fp4("w1", w1_raw)
+
+        yv = [tile("yv_sb%d" % t, [P, S], F32) for t in range(PACK)]
+        vs = [tile("vs%d" % t, [P, S], F32) for t in range(PACK)]
+
+        def empty_yv(t):
+            nc.scalar.activation(yv[t][:], yv_ps[t][:], ACT.Copy, scale=half_unit[:, t : t + 1])
+
+        def fetch_vs(t):
+            for cols, offsets in halves(sec_t):
+                nc.scalar.activation(vs[t][:, cols], yv[t][:].indirect(offsets), ACT.Copy)
+
+        for t in range(PACK):
+            empty_yv(t)
+        for t in range(PACK):
+            fetch_vs(t)
+
+        hid2_bf = tile("hid2_bf", [P, Z, PACK], BF16)
+        for c in range(4):
+            cols = slice(P * c, P * (c + 1))
+            ye_ps = bank(c, "ye%d" % c, [P, PACK, P])
+            for t in range(PACK):
+                product(ye_ps[:, t, :], w3, ws3, t, ew[:, cols], es[:, cols])
+            nc.vector.tensor_tensor(
+                hid2_bf[:, cols, :],
+                ye_ps[:].rearrange("p t n -> p n t"),
+                units[:, 4:8].unsqueeze(1).to_broadcast([P, P, PACK]),
+                ALU.mult,
+            )
+
+        y_ps = [bank(4 + t, "y%d" % t, [P, S]) for t in range(PACK)]
+        for t in range(PACK):
+            product(y_ps[t][:], w1, ws1, t, xw[:], xs[:])
+
+        planes = tile("planes", [P, PACK, PACK, P], BF16)
+
+        def combine(t):
+            nc.vector.scalar_tensor_tensor(
+                planes[:, t].rearrange("p r m -> p m r"),
+                y_ps[t][:].rearrange("p (m r) -> p m r", r=PACK),
+                units[:, t : t + 1],
+                vs[t][:].rearrange("p (m r) -> p m r", r=PACK),
+                ALU.mult,
+                ALU.add,
+            )
+
+        hid2_w = tile("hid2_w", [P, Z], U32)
+        hid2_s = tile("hid2_s", [P, Z], U8)
+        combine(0)
+        nc.vector.quantize_mx(hid2_w[:].bitcast(FP8X4), hid2_s[:], hid2_bf[:].rearrange("p c t -> p (c t)"))
+        for t in range(1, PACK):
+            combine(t)
+
+        hid_bf = [tile("hid_bf%d" % r, [P, P, PACK], BF16) for r in range(PACK)]
+        hid_w = [tile("hid_w%d" % r, [P, P], U32) for r in range(PACK)]
+        hid_s = [tile("hid_s%d" % r, [P, P], U8) for r in range(PACK)]
+
+        def weave(r, copy):
+            copy(
+                hid_bf[r][:].rearrange("p (c i) t -> p c t i", i=4),
+                planes[:, :, r, :].rearrange("p t (c i) -> p c t i", i=4),
+            )
+
+        def quantise(r):
+            nc.vector.quantize_mx(hid_w[r][:].bitcast(FP8X4), hid_s[r][:], hid_bf[r][:].rearrange("p c t -> p (c t)"))
+
+        weave(3, nc.scalar.copy)
+        weave(0, nc.vector.tensor_copy)
+        weave(1, nc.vector.tensor_copy)
+        quantise(0)
+        weave(2, nc.vector.tensor_copy)
+        for r in range(1, PACK):
+            quantise(r)
+
+        sc_ps = [bank(r, "sc%d" % r, [P, Z]) for r in range(PACK)]
+        for r in range(PACK):
+            nc.tensor.matmul_mx(
+                sc_ps[r][:], lhsT=hid_w[r][:].bitcast(FP8X4), lhsT_scale=hid_s[r][:],
+                rhs=hid2_w[:].bitcast(FP8X4), rhs_scale=hid2_s[:], start=True, stop=True,
+            )
+
+        beta = [tile("beta%d" % r, [P, Z], F32) for r in range(PACK)]
+        other = [tile("other%d" % r, [P, Z], F32) for r in range(PACK)]
+        prod = [tile("prod%d" % r, [P, Z], F32) for r in range(PACK)]
+        expl = [tile("expl%d" % r, [P, 1], F32) for r in range(PACK)]
+        neg_expl = [tile("neg_expl%d" % r, [P, 1], F32) for r in range(2, PACK)]
+        squares = tile("squares", [P, Z], BF16)
+        res = tile("res", [P, PACK, Z], F32)
+        out_rows = out_0.rearrange("(p r) e -> p r e", r=PACK)
+
+        for r in range(PACK):
+            nc.vector.tensor_tensor(beta[r][:], sc_ps[r][:], inv_vol[:], ALU.mult)
+
+        def mean_square(r):
+            nc.scalar.activation(squares[:], beta[r][:], ACT.Square, scale=Z ** -0.5, accum_out=expl[r][:])
+
+        for r in range(2):
+            mean_square(r)
+            for cols, offsets in halves(prx_t):
+                nc.scalar.activation(other[r][:, cols], beta[r][:].indirect(offsets), ACT.Copy)
+        for r in range(2, PACK):
+            mean_square(r)
+            nc.scalar.activation(neg_expl[r - 2][:], expl[r][:], ACT.Copy, scale=-1.0)
+        for r in range(2, PACK):
+            nc.vector.tensor_copy(other[r][:], beta[r][:])
+        for r in range(2, PACK):
+            for cols, offsets in halves(prx_t):
+                nc.vector.tensor_tensor(prod[r][:, cols], beta[r][:].indirect(offsets), other[r][:, cols], ALU.mult)
+            nc.scalar.activation(res[:, r, :], prod[r][:], ACT.Identity, bias=neg_expl[r - 2][:])
+            nc.sync.dma_start(out_rows[:, r, :], res[:, r, :])
+        for r in range(2):
+            nc.vector.tensor_tensor(prod[r][:], other[r][:], beta[r][:], ALU.mult)
+        for r in range(2):
+            nc.vector.tensor_scalar(res[:, r, :], prod[r][:], expl[r][:], None, ALU.subtract)
+            nc.sync.dma_start(out_rows[:, r, :], res[:, r, :])
+
+        res_bf = tile("res_bf", [P, Z, PACK], BF16)
+        for cols, copy in ((slice(0, SPLIT), nc.vector.tensor_copy), (slice(SPLIT, Z), nc.scalar.copy)):
+            copy(
+                res_bf[:, cols, :].rearrange("p (c i) r -> p c r i", i=4),
+                res[:, :, cols].rearrange("p r (c i) -> p c r i", i=4),
+            )
+        res_w = tile("res_w", [P, Z], U32)
+        res_s = tile("res_s", [P, Z], U8)
+        nc.vector.quantize_mx(res_w[:].bitcast(FP8X4), res_s[:], res_bf[:].rearrange("p c r -> p (c r)"))
+        nc.sync.dma_start(out_1[0].rearrange("p c r -> p (c r)").bitcast(I32), res_w[:].bitcast(I32))
+        for q in range(4):
+            (nc.scalar, nc.sync)[q % 2].dma_start(out_2[0, 4 * q : 4 * q + 4, :].bitcast(I32), res_s[QUAD * q : QUAD * q + 4, :].bitcast(I32))

@@ -59,7 +59,7 @@ def tile_picked_yfcovr_cross_po_kernel(
             return t
 
         def load_fp4(name, src):
-            t = tile(name, [P, 2 * H], U8)
+            t = sb.tile([P, 2 * H], U8, name=name, tag=name, align_bytes=64)
             nc.sync.dma_start(t[:].bitcast(I32), src[0].bitcast(I32))
             return t
 
@@ -83,33 +83,36 @@ def tile_picked_yfcovr_cross_po_kernel(
             return [(slice(h * HALF, (h + 1) * HALF), offsets[:, 16 * h : 16 * (h + 1)]) for h in range(2)]
 
         xs_all = cleared("xs_all", T)
-        rows = tile("rows", [P, P], F32)
-        nc.vector.memset(rows[:], 0.0)
         ws_raw = cleared("ws_raw", 3 * H)
         ws1_raw, ws2_raw, ws3_raw = (ws_raw[:, i * H : (i + 1) * H] for i in range(3))
+        rows = tile("rows", [P, 2, P], F32)
+        nc.vector.memset(rows[:], 0.0)
         es_all = cleared("es_all", W)
-        for i, src in enumerate((unit, unit2)):
-            nc.gpsimd.dma_start(
-                rows[4 * i : 4 * i + 4, :].rearrange("t (g r) -> t g r", r=8),
-                src.rearrange("(g t r) o -> t g (r o)", t=PACK, r=8),
-            )
         ident = tile("ident", [P, P], F32)
         make_identity(nc, ident[:])
-        load_scale_rows(ws1_raw, w1_scales, (nc.gpsimd,) * 4)
+
+        def load_unit(queue, i, src):
+            queue.dma_start(
+                rows[0:PACK, i, :].rearrange("t (g r) -> t g r", r=8),
+                src.rearrange("(g t r) o -> t g (r o)", t=PACK, r=8),
+            )
 
         offs_t = load_list("offs_t", offs)
         vol_col = tile("vol_col", [P, 8], F32)
         nc.scalar.dma_start(vol_col[:], vol[0].rearrange("(p c) -> p c", c=8))
         load_scale_rows(xs_all[:], x_scales, (nc.sync, nc.sync, nc.scalar, nc.scalar))
         xw_all = load_words("xw_all", x_words, T)
-        w2_raw = load_fp4("w2_raw", w2_words)
-        load_scale_rows(ws2_raw, w2_scales, (nc.scalar, nc.scalar, nc.scalar, nc.sync))
+        load_scale_rows(ws2_raw, w2_scales, (nc.scalar,) * 4)
+        load_unit(nc.scalar, 0, unit)
         hdg_t = load_list("hdg_t", hdg)
-        ew_all = load_words("ew_all", e_words, W)
+        w2_raw = load_fp4("w2_raw", w2_words)
         load_scale_rows(es_all[:], e_scales, (nc.sync,) * 4)
+        ew_all = load_words("ew_all", e_words, W)
         sec_t = load_list("sec_t", sec)
         load_scale_rows(ws3_raw, w3_scales, (nc.sync,) * 4)
         w3_raw = load_fp4("w3_raw", w3_words)
+        load_unit(nc.sync, 1, unit2)
+        load_scale_rows(ws1_raw, w1_scales, (nc.sync,) * 4)
         w1_raw = load_fp4("w1_raw", w1_words)
         prx_t = load_list("prx_t", prx)
 
@@ -126,11 +129,11 @@ def tile_picked_yfcovr_cross_po_kernel(
                 nc.tensor.transpose(spread[:, c, :], inv_col[:, col : col + 1].to_broadcast([P, P]), ident[:])
             nc.scalar.activation(inv_all[:, :, 4 * b : 4 * b + 4], spread[:].rearrange("p c n -> p n c"), ACT.Copy)
         turned = bank(7, "turned", [P, P])
-        nc.tensor.transpose(turned[:], rows[:], ident[:])
-        units = tile("units", [P, 8], F32)
+        nc.tensor.transpose(turned[:], rows[:, 0, :], ident[:])
+        unit_col = tile("unit_col", [P, PACK], F32)
         half_unit = tile("half_unit", [P, PACK], F32)
-        nc.scalar.activation(half_unit[:], turned[:, 0:4], ACT.Copy, scale=0.5)
-        nc.scalar.activation(units[:], turned[:, 0:8], ACT.Copy)
+        nc.scalar.activation(half_unit[:], turned[:, 0:PACK], ACT.Copy, scale=0.5)
+        nc.scalar.activation(unit_col[:], turned[:, 0:PACK], ACT.Copy)
         inv_vol = tile("inv_vol", [P, Z], F32)
         nc.scalar.activation(inv_vol[:], inv_all[:].rearrange("p n c -> p (n c)").indirect(hdg_t[:]), ACT.Copy)
 
@@ -154,12 +157,16 @@ def tile_picked_yfcovr_cross_po_kernel(
         for t in range(PACK):
             product(yv_ps[t][:], w2, ws2, t, xw[:], xs[:])
 
-        ew = tile("ew", [P, Z], U32)
-        nc.vector.tensor_copy(ew[:], ew_all[:].indirect(hdg_t[:]))
         es = tile("es", [P, Z], U8)
         nc.vector.tensor_copy(es[:], es_all[:].indirect(hdg_t[:]))
+        ew = tile("ew", [P, Z], U32)
+        nc.vector.tensor_copy(ew[:], ew_all[:].indirect(hdg_t[:]))
         ws3 = deal_scales("ws3", ws3_raw)
         w3 = deal_fp4("w3", w3_raw)
+        turned2 = bank(7, "turned2", [P, P])
+        nc.tensor.transpose(turned2[:], rows[:, 1, :], ident[:])
+        unit2_col = tile("unit2_col", [P, PACK], F32)
+        nc.vector.tensor_copy(unit2_col[:], turned2[:, 0:PACK])
         ws1 = deal_scales("ws1", ws1_raw)
         w1 = deal_fp4("w1", w1_raw)
 
@@ -178,18 +185,29 @@ def tile_picked_yfcovr_cross_po_kernel(
         for t in range(PACK):
             fetch_vs(t)
 
-        hid2_bf = tile("hid2_bf", [P, Z, PACK], BF16)
+        front_bf = tile("front_bf", [P, 2 * P, PACK], BF16)
+        third_bf = sb.tile([P, P, PACK], BF16, name="third_bf", tag="w1_raw", align_bytes=64)
+        last_bf = tile("last_bf", [P, P, PACK], BF16)
+        last_planes = tile("last_planes", [P, PACK, P], BF16)
         for c in range(4):
             cols = slice(P * c, P * (c + 1))
             ye_ps = bank(c, "ye%d" % c, [P, PACK, P])
             for t in range(PACK):
                 product(ye_ps[:, t, :], w3, ws3, t, ew[:, cols], es[:, cols])
-            nc.vector.tensor_tensor(
-                hid2_bf[:, cols, :],
-                ye_ps[:].rearrange("p t n -> p n t"),
-                units[:, 4:8].unsqueeze(1).to_broadcast([P, P, PACK]),
-                ALU.mult,
-            )
+            if c < 3:
+                nc.vector.tensor_tensor(
+                    front_bf[:, cols, :] if c < 2 else third_bf[:],
+                    ye_ps[:].rearrange("p t n -> p n t"),
+                    unit2_col[:].unsqueeze(1).to_broadcast([P, P, PACK]),
+                    ALU.mult,
+                )
+            else:
+                for t in range(PACK):
+                    nc.scalar.activation(last_planes[:, t, :], ye_ps[:, t, :], ACT.Copy, scale=unit2_col[:, t : t + 1])
+                nc.scalar.copy(
+                    last_bf[:].rearrange("p (c i) t -> p c t i", i=4),
+                    last_planes[:].rearrange("p t (c i) -> p c t i", i=4),
+                )
 
         y_ps = [bank(4 + t, "y%d" % t, [P, S]) for t in range(PACK)]
         for t in range(PACK):
@@ -201,7 +219,7 @@ def tile_picked_yfcovr_cross_po_kernel(
             nc.vector.scalar_tensor_tensor(
                 planes[:, t].rearrange("p r m -> p m r"),
                 y_ps[t][:].rearrange("p (m r) -> p m r", r=PACK),
-                units[:, t : t + 1],
+                unit_col[:, t : t + 1],
                 vs[t][:].rearrange("p (m r) -> p m r", r=PACK),
                 ALU.mult,
                 ALU.add,
@@ -209,10 +227,16 @@ def tile_picked_yfcovr_cross_po_kernel(
 
         hid2_w = tile("hid2_w", [P, Z], U32)
         hid2_s = tile("hid2_s", [P, Z], U8)
+
+        def quantise2(cols, src):
+            nc.vector.quantize_mx(hid2_w[:, cols].bitcast(FP8X4), hid2_s[:, cols], src[:].rearrange("p c t -> p (c t)"))
+
+        quantise2(slice(0, 2 * P), front_bf)
         combine(0)
-        nc.vector.quantize_mx(hid2_w[:].bitcast(FP8X4), hid2_s[:], hid2_bf[:].rearrange("p c t -> p (c t)"))
+        quantise2(slice(2 * P, 3 * P), third_bf)
         for t in range(1, PACK):
             combine(t)
+        quantise2(slice(3 * P, 4 * P), last_bf)
 
         hid_bf = [tile("hid_bf%d" % r, [P, P, PACK], BF16) for r in range(PACK)]
         hid_w = [tile("hid_w%d" % r, [P, P], U32) for r in range(PACK)]

@@ -22,6 +22,7 @@ PACK = 4
 QUAD = 32
 HALF = 256
 SPLIT = 320
+WEAVE = 45
 
 
 def tile_picked_yfcovr_cross_po_kernel(
@@ -58,9 +59,9 @@ def tile_picked_yfcovr_cross_po_kernel(
             nc.sync.dma_start(t[:].bitcast(I32), src[0].rearrange("p c r -> p (c r)").bitcast(I32))
             return t
 
-        def load_fp4(name, src):
+        def load_fp4(name, src, queue):
             t = sb.tile([P, 2 * H], U8, name=name, tag=name, align_bytes=64)
-            nc.sync.dma_start(t[:].bitcast(I32), src[0].bitcast(I32))
+            queue.dma_start(t[:].bitcast(I32), src[0].bitcast(I32))
             return t
 
         def deal_fp4(name, raw):
@@ -75,45 +76,49 @@ def tile_picked_yfcovr_cross_po_kernel(
             t = tile(name, [P, H], U8)
             nc.vector.tensor_copy(
                 t[:].bitcast(I32).rearrange("p (t g c) -> p t g c", t=PACK, c=2),
-                raw.bitcast(I32).rearrange("p (g t c) -> p t g c", t=PACK, c=2),
+                raw[:].bitcast(I32).rearrange("p (g t c) -> p t g c", t=PACK, c=2),
             )
             return t
 
         def halves(offsets):
             return [(slice(h * HALF, (h + 1) * HALF), offsets[:, 16 * h : 16 * (h + 1)]) for h in range(2)]
 
-        xs_all = cleared("xs_all", T)
-        ws_raw = cleared("ws_raw", 3 * H)
-        ws1_raw, ws2_raw, ws3_raw = (ws_raw[:, i * H : (i + 1) * H] for i in range(3))
-        rows = tile("rows", [P, 2, P], F32)
-        nc.vector.memset(rows[:], 0.0)
-        es_all = cleared("es_all", W)
-        ident = tile("ident", [P, P], F32)
-        make_identity(nc, ident[:])
-
-        def load_unit(queue, i, src):
+        def load_unit(name, queue, src):
+            t = tile(name, [P, P], F32)
+            nc.gpsimd.memset(t[:], 0.0)
             queue.dma_start(
-                rows[0:PACK, i, :].rearrange("t (g r) -> t g r", r=8),
+                t[0:PACK, :].rearrange("t (g r) -> t g r", r=8),
                 src.rearrange("(g t r) o -> t g (r o)", t=PACK, r=8),
             )
+            return t
+
+        ws2_raw = cleared("ws2_raw", H)
+        es_all = cleared("es_all", W)
+        ws3_raw = cleared("ws3_raw", H)
+        ws1_raw = cleared("ws1_raw", H)
+        unit_rows = load_unit("unit_rows", nc.gpsimd, unit)
+        ident = tile("ident", [P, P], F32)
+        make_identity(nc, ident[:])
 
         offs_t = load_list("offs_t", offs)
         vol_col = tile("vol_col", [P, 8], F32)
         nc.scalar.dma_start(vol_col[:], vol[0].rearrange("(p c) -> p c", c=8))
-        load_scale_rows(xs_all[:], x_scales, (nc.sync, nc.sync, nc.scalar, nc.scalar))
+        xs_all = tile("xs_all", [P, T], U8)
+        for q, queue in enumerate((nc.sync, nc.sync, nc.scalar, nc.scalar)):
+            rows4 = x_scales[0, 4 * q : 4 * q + 4, :].bitcast(I32)
+            queue.dma_start(xs_all[QUAD * q : QUAD * (q + 1), :].bitcast(I32), rows4.partition_broadcast(8))
         xw_all = load_words("xw_all", x_words, T)
-        load_scale_rows(ws2_raw, w2_scales, (nc.scalar,) * 4)
-        load_unit(nc.scalar, 0, unit)
+        w2_raw = load_fp4("w2_raw", w2_words, nc.scalar)
         hdg_t = load_list("hdg_t", hdg)
-        w2_raw = load_fp4("w2_raw", w2_words)
-        load_scale_rows(es_all[:], e_scales, (nc.sync,) * 4)
+        load_scale_rows(ws2_raw[:], w2_scales, (nc.sync,) * 4)
         ew_all = load_words("ew_all", e_words, W)
+        load_scale_rows(es_all[:], e_scales, (nc.sync,) * 4)
+        unit2_rows = load_unit("unit2_rows", nc.sync, unit2)
+        load_scale_rows(ws3_raw[:], w3_scales, (nc.sync,) * 4)
+        w3_raw = load_fp4("w3_raw", w3_words, nc.sync)
         sec_t = load_list("sec_t", sec)
-        load_scale_rows(ws3_raw, w3_scales, (nc.sync,) * 4)
-        w3_raw = load_fp4("w3_raw", w3_words)
-        load_unit(nc.sync, 1, unit2)
-        load_scale_rows(ws1_raw, w1_scales, (nc.sync,) * 4)
-        w1_raw = load_fp4("w1_raw", w1_words)
+        load_scale_rows(ws1_raw[:], w1_scales, (nc.sync,) * 4)
+        w1_raw = load_fp4("w1_raw", w1_words, nc.sync)
         prx_t = load_list("prx_t", prx)
 
         inv_col = tile("inv_col", [P, 8], F32)
@@ -129,7 +134,7 @@ def tile_picked_yfcovr_cross_po_kernel(
                 nc.tensor.transpose(spread[:, c, :], inv_col[:, col : col + 1].to_broadcast([P, P]), ident[:])
             nc.scalar.activation(inv_all[:, :, 4 * b : 4 * b + 4], spread[:].rearrange("p c n -> p n c"), ACT.Copy)
         turned = bank(7, "turned", [P, P])
-        nc.tensor.transpose(turned[:], rows[:, 0, :], ident[:])
+        nc.tensor.transpose(turned[:], unit_rows[:], ident[:])
         unit_col = tile("unit_col", [P, PACK], F32)
         half_unit = tile("half_unit", [P, PACK], F32)
         nc.scalar.activation(half_unit[:], turned[:, 0:PACK], ACT.Copy, scale=0.5)
@@ -137,10 +142,10 @@ def tile_picked_yfcovr_cross_po_kernel(
         inv_vol = tile("inv_vol", [P, Z], F32)
         nc.scalar.activation(inv_vol[:], inv_all[:].rearrange("p n c -> p (n c)").indirect(hdg_t[:]), ACT.Copy)
 
+        w2 = deal_fp4("w2", w2_raw)
         xw = tile("xw", [P, S], U32)
         nc.vector.tensor_copy(xw[:], xw_all[:].indirect(offs_t[:]))
         ws2 = deal_scales("ws2", ws2_raw)
-        w2 = deal_fp4("w2", w2_raw)
 
         def product(out, w, w_scales, t, words, scales):
             nc.tensor.matmul_mx(
@@ -157,21 +162,21 @@ def tile_picked_yfcovr_cross_po_kernel(
         for t in range(PACK):
             product(yv_ps[t][:], w2, ws2, t, xw[:], xs[:])
 
-        es = tile("es", [P, Z], U8)
-        nc.vector.tensor_copy(es[:], es_all[:].indirect(hdg_t[:]))
         ew = tile("ew", [P, Z], U32)
         nc.vector.tensor_copy(ew[:], ew_all[:].indirect(hdg_t[:]))
-        ws3 = deal_scales("ws3", ws3_raw)
-        w3 = deal_fp4("w3", w3_raw)
+        es = tile("es", [P, Z], U8)
+        nc.vector.tensor_copy(es[:], es_all[:].indirect(hdg_t[:]))
         turned2 = bank(7, "turned2", [P, P])
-        nc.tensor.transpose(turned2[:], rows[:, 1, :], ident[:])
+        nc.tensor.transpose(turned2[:], unit2_rows[:], ident[:])
         unit2_col = tile("unit2_col", [P, PACK], F32)
         nc.vector.tensor_copy(unit2_col[:], turned2[:, 0:PACK])
+        ws3 = deal_scales("ws3", ws3_raw)
+        w3 = deal_fp4("w3", w3_raw)
         ws1 = deal_scales("ws1", ws1_raw)
         w1 = deal_fp4("w1", w1_raw)
 
         yv = [tile("yv_sb%d" % t, [P, S], F32) for t in range(PACK)]
-        vs = [tile("vs%d" % t, [P, S], F32) for t in range(PACK)]
+        vs = [sb.tile([P, S], F32, name="vs%d" % t, tag="vs%d" % t, align_bytes=64) for t in range(PACK)]
 
         def empty_yv(t):
             nc.scalar.activation(yv[t][:], yv_ps[t][:], ACT.Copy, scale=half_unit[:, t : t + 1])
@@ -188,39 +193,31 @@ def tile_picked_yfcovr_cross_po_kernel(
         front_bf = tile("front_bf", [P, 2 * P, PACK], BF16)
         third_bf = sb.tile([P, P, PACK], BF16, name="third_bf", tag="w1_raw", align_bytes=64)
         last_bf = tile("last_bf", [P, P, PACK], BF16)
-        last_planes = tile("last_planes", [P, PACK, P], BF16)
+        ye_ps = [bank(c, "ye%d" % c, [P, PACK, P]) for c in range(4)]
         for c in range(4):
             cols = slice(P * c, P * (c + 1))
-            ye_ps = bank(c, "ye%d" % c, [P, PACK, P])
             for t in range(PACK):
-                product(ye_ps[:, t, :], w3, ws3, t, ew[:, cols], es[:, cols])
+                product(ye_ps[c][:, t, :], w3, ws3, t, ew[:, cols], es[:, cols])
             if c < 3:
                 nc.vector.tensor_tensor(
                     front_bf[:, cols, :] if c < 2 else third_bf[:],
-                    ye_ps[:].rearrange("p t n -> p n t"),
+                    ye_ps[c][:].rearrange("p t n -> p n t"),
                     unit2_col[:].unsqueeze(1).to_broadcast([P, P, PACK]),
                     ALU.mult,
-                )
-            else:
-                for t in range(PACK):
-                    nc.scalar.activation(last_planes[:, t, :], ye_ps[:, t, :], ACT.Copy, scale=unit2_col[:, t : t + 1])
-                nc.scalar.copy(
-                    last_bf[:].rearrange("p (c i) t -> p c t i", i=4),
-                    last_planes[:].rearrange("p t (c i) -> p c t i", i=4),
                 )
 
         y_ps = [bank(4 + t, "y%d" % t, [P, S]) for t in range(PACK)]
         for t in range(PACK):
             product(y_ps[t][:], w1, ws1, t, xw[:], xs[:])
 
-        planes = tile("planes", [P, PACK, PACK, P], BF16)
+        planes = tile("planes", [P, PACK, S], BF16)
 
         def combine(t):
             nc.vector.scalar_tensor_tensor(
-                planes[:, t].rearrange("p r m -> p m r"),
-                y_ps[t][:].rearrange("p (m r) -> p m r", r=PACK),
+                planes[:, t, :],
+                y_ps[t][:],
                 unit_col[:, t : t + 1],
-                vs[t][:].rearrange("p (m r) -> p m r", r=PACK),
+                vs[t][:],
                 ALU.mult,
                 ALU.add,
             )
@@ -233,31 +230,28 @@ def tile_picked_yfcovr_cross_po_kernel(
 
         quantise2(slice(0, 2 * P), front_bf)
         combine(0)
+        last_planes = sb.tile([P, PACK, P], BF16, name="last_planes", tag="vs0", align_bytes=64)
+        for t in range(PACK):
+            nc.scalar.activation(last_planes[:, t, :], ye_ps[3][:, t, :], ACT.Copy, scale=unit2_col[:, t : t + 1])
+        nc.scalar.copy(
+            last_bf[:].rearrange("p (c i) t -> p c t i", i=4),
+            last_planes[:].rearrange("p t (c i) -> p c t i", i=4),
+        )
         quantise2(slice(2 * P, 3 * P), third_bf)
         for t in range(1, PACK):
             combine(t)
         quantise2(slice(3 * P, 4 * P), last_bf)
 
-        hid_bf = [tile("hid_bf%d" % r, [P, P, PACK], BF16) for r in range(PACK)]
+        hid_bf = tile("hid_bf", [P, PACK, P, PACK], BF16)
         hid_w = [tile("hid_w%d" % r, [P, P], U32) for r in range(PACK)]
         hid_s = [tile("hid_s%d" % r, [P, P], U8) for r in range(PACK)]
-
-        def weave(r, copy):
+        for pairs, copy in ((slice(0, WEAVE), nc.vector.tensor_copy), (slice(WEAVE, P // 2), nc.scalar.copy)):
             copy(
-                hid_bf[r][:].rearrange("p (c i) t -> p c t i", i=4),
-                planes[:, :, r, :].rearrange("p t (c i) -> p c t i", i=4),
+                hid_bf[:].rearrange("p r (a b) t -> p a r b t", b=2)[:, pairs],
+                planes[:].rearrange("p t (a b r) -> p a r b t", b=2, r=PACK)[:, pairs],
             )
-
-        def quantise(r):
-            nc.vector.quantize_mx(hid_w[r][:].bitcast(FP8X4), hid_s[r][:], hid_bf[r][:].rearrange("p c t -> p (c t)"))
-
-        weave(3, nc.scalar.copy)
-        weave(0, nc.vector.tensor_copy)
-        weave(1, nc.vector.tensor_copy)
-        quantise(0)
-        weave(2, nc.vector.tensor_copy)
-        for r in range(1, PACK):
-            quantise(r)
+        for r in range(PACK):
+            nc.vector.quantize_mx(hid_w[r][:].bitcast(FP8X4), hid_s[r][:], hid_bf[:, r].rearrange("p c t -> p (c t)"))
 
         sc_ps = [bank(r, "sc%d" % r, [P, Z]) for r in range(PACK)]
         for r in range(PACK):
@@ -302,14 +296,22 @@ def tile_picked_yfcovr_cross_po_kernel(
             nc.sync.dma_start(out_rows[:, r, :], res[:, r, :])
 
         res_bf = tile("res_bf", [P, Z, PACK], BF16)
-        for cols, copy in ((slice(0, SPLIT), nc.vector.tensor_copy), (slice(SPLIT, Z), nc.scalar.copy)):
+        shares = (
+            (slice(0, HALF), nc.vector.tensor_copy),
+            (slice(HALF, SPLIT), nc.vector.tensor_copy),
+            (slice(SPLIT, Z), nc.scalar.copy),
+        )
+        for cols, copy in shares:
             copy(
                 res_bf[:, cols, :].rearrange("p (c i) r -> p c r i", i=4),
                 res[:, :, cols].rearrange("p r (c i) -> p c r i", i=4),
             )
         res_w = tile("res_w", [P, Z], U32)
         res_s = tile("res_s", [P, Z], U8)
-        nc.vector.quantize_mx(res_w[:].bitcast(FP8X4), res_s[:], res_bf[:].rearrange("p c r -> p (c r)"))
-        nc.sync.dma_start(out_1[0].rearrange("p c r -> p (c r)").bitcast(I32), res_w[:].bitcast(I32))
+        out_words = out_1[0].rearrange("p c r -> p (c r)").bitcast(I32)
+        for h in range(2):
+            cols = slice(h * HALF, (h + 1) * HALF)
+            nc.vector.quantize_mx(res_w[:, cols].bitcast(FP8X4), res_s[:, cols], res_bf[:, cols, :].rearrange("p c r -> p (c r)"))
+            nc.sync.dma_start(out_words[:, cols], res_w[:, cols].bitcast(I32))
         for q in range(4):
             (nc.scalar, nc.sync)[q % 2].dma_start(out_2[0, 4 * q : 4 * q + 4, :].bitcast(I32), res_s[QUAD * q : QUAD * q + 4, :].bitcast(I32))

@@ -46,7 +46,7 @@ def tile_picked_yfcovr_cross_po_kernel(
             return t
 
         def cleared(name, cols):
-            t = tile(name, [P, cols], U8)
+            t = sb.tile([P, cols], U8, name=name, tag=name, align_bytes=64)
             nc.vector.memset(t[:].bitcast(I32), 0)
             return t
 
@@ -114,8 +114,8 @@ def tile_picked_yfcovr_cross_po_kernel(
         ew_all = load_words("ew_all", e_words, W)
         load_scale_rows(es_all[:], e_scales, (nc.sync,) * 4)
         unit2_rows = load_unit("unit2_rows", nc.sync, unit2)
-        load_scale_rows(ws3_raw[:], w3_scales, (nc.sync,) * 4)
         w3_raw = load_fp4("w3_raw", w3_words, nc.sync)
+        load_scale_rows(ws3_raw[:], w3_scales, (nc.sync,) * 4)
         sec_t = load_list("sec_t", sec)
         load_scale_rows(ws1_raw[:], w1_scales, (nc.sync,) * 4)
         w1_raw = load_fp4("w1_raw", w1_words, nc.sync)
@@ -164,14 +164,16 @@ def tile_picked_yfcovr_cross_po_kernel(
 
         ew = tile("ew", [P, Z], U32)
         nc.vector.tensor_copy(ew[:], ew_all[:].indirect(hdg_t[:]))
-        es = tile("es", [P, Z], U8)
-        nc.vector.tensor_copy(es[:], es_all[:].indirect(hdg_t[:]))
+        es_front = tile("es_front", [P, HALF], U8)
+        nc.vector.tensor_copy(es_front[:], es_all[:].indirect(hdg_t[:, 0:16]))
         turned2 = bank(7, "turned2", [P, P])
         nc.tensor.transpose(turned2[:], unit2_rows[:], ident[:])
         unit2_col = tile("unit2_col", [P, PACK], F32)
         nc.vector.tensor_copy(unit2_col[:], turned2[:, 0:PACK])
-        ws3 = deal_scales("ws3", ws3_raw)
         w3 = deal_fp4("w3", w3_raw)
+        ws3 = deal_scales("ws3", ws3_raw)
+        es_back = sb.tile([P, HALF], U8, name="es_back", tag="ws3_raw", align_bytes=64)
+        nc.vector.tensor_copy(es_back[:], es_all[:].indirect(hdg_t[:, 16:32]))
         ws1 = deal_scales("ws1", ws1_raw)
         w1 = deal_fp4("w1", w1_raw)
 
@@ -196,8 +198,9 @@ def tile_picked_yfcovr_cross_po_kernel(
         ye_ps = [bank(c, "ye%d" % c, [P, PACK, P]) for c in range(4)]
         for c in range(4):
             cols = slice(P * c, P * (c + 1))
+            es = (es_front, es_back)[c // 2][:, P * (c % 2) : P * (c % 2 + 1)]
             for t in range(PACK):
-                product(ye_ps[c][:, t, :], w3, ws3, t, ew[:, cols], es[:, cols])
+                product(ye_ps[c][:, t, :], w3, ws3, t, ew[:, cols], es)
             if c < 3:
                 nc.vector.tensor_tensor(
                     front_bf[:, cols, :] if c < 2 else third_bf[:],
@@ -264,34 +267,36 @@ def tile_picked_yfcovr_cross_po_kernel(
         other = [tile("other%d" % r, [P, Z], F32) for r in range(PACK)]
         prod = [tile("prod%d" % r, [P, Z], F32) for r in range(PACK)]
         expl = [tile("expl%d" % r, [P, 1], F32) for r in range(PACK)]
-        neg_expl = [tile("neg_expl%d" % r, [P, 1], F32) for r in range(2, PACK)]
+        neg_expl = tile("neg_expl", [P, 1], F32)
         squares = tile("squares", [P, Z], BF16)
         res = tile("res", [P, PACK, Z], F32)
         out_rows = out_0.rearrange("(p r) e -> p r e", r=PACK)
+        by_vector, by_scalar = (0, 1), (2, 3)
 
         for r in range(PACK):
             nc.vector.tensor_tensor(beta[r][:], sc_ps[r][:], inv_vol[:], ALU.mult)
+        for r in by_vector:
+            nc.gpsimd.tensor_scalar(other[r][:], beta[r][:], 1.0, 0.0, ALU.mult, ALU.add)
 
         def mean_square(r):
             nc.scalar.activation(squares[:], beta[r][:], ACT.Square, scale=Z ** -0.5, accum_out=expl[r][:])
 
-        for r in range(2):
-            mean_square(r)
+        mean_square(0)
+        nc.scalar.activation(neg_expl[:], expl[0][:], ACT.Copy, scale=-1.0)
+        mean_square(1)
+        for r in by_scalar:
             for cols, offsets in halves(prx_t):
                 nc.scalar.activation(other[r][:, cols], beta[r][:].indirect(offsets), ACT.Copy)
-        for r in range(2, PACK):
+        for r in by_scalar:
             mean_square(r)
-            nc.scalar.activation(neg_expl[r - 2][:], expl[r][:], ACT.Copy, scale=-1.0)
-        for r in range(2, PACK):
-            nc.vector.tensor_copy(other[r][:], beta[r][:])
-        for r in range(2, PACK):
+        for r in by_vector:
             for cols, offsets in halves(prx_t):
                 nc.vector.tensor_tensor(prod[r][:, cols], beta[r][:].indirect(offsets), other[r][:, cols], ALU.mult)
-            nc.scalar.activation(res[:, r, :], prod[r][:], ACT.Identity, bias=neg_expl[r - 2][:])
-            nc.sync.dma_start(out_rows[:, r, :], res[:, r, :])
-        for r in range(2):
+        for r in by_scalar:
             nc.vector.tensor_tensor(prod[r][:], other[r][:], beta[r][:], ALU.mult)
-        for r in range(2):
+        nc.scalar.activation(res[:, 0, :], prod[0][:], ACT.Identity, bias=neg_expl[:])
+        nc.sync.dma_start(out_rows[:, 0, :], res[:, 0, :])
+        for r in range(1, PACK):
             nc.vector.tensor_scalar(res[:, r, :], prod[r][:], expl[r][:], None, ALU.subtract)
             nc.sync.dma_start(out_rows[:, r, :], res[:, r, :])
 

from contextlib import ExitStack

import concourse.mybir as mybir
from concourse.masks import make_identity

K, T, S, H, Z, W = 512, 2048, 512, 512, 512, 1024
FLOPS = 4 * 2 * 512 * 512 * 512

F32 = mybir.dt.float32
BF16 = mybir.dt.bfloat16
I32 = mybir.dt.int32
U32 = mybir.dt.uint32
U16 = mybir.dt.uint16
U8 = mybir.dt.uint8
FP8X4 = mybir.dt.float8_e4m3fn_x4
FP4X4 = mybir.dt.float4_e2m1fn_x4
ALU = mybir.AluOpType
ACT = mybir.ActivationFunctionType

P = 128
PACK = 4
QUAD = 32
HALF = 256
SPLIT = 320
WEAVE = 45


def tile_picked_yfcovr_cross_po_kernel(
    tc, x_words, x_scales, w1_words, w1_scales, w2_words, w2_scales, e_words, e_scales, w3_words, w3_scales,
    unit, unit2, vol, offs, hdg, sec, prx, out_0, out_1, out_2,
):
    nc = tc.nc
    with ExitStack() as ctx:
        sb = ctx.enter_context(tc.tile_pool(name="sb", bufs=1))
        ps = ctx.enter_context(tc.psum_pool(name="ps", bufs=1))

        def tile(name, shape, dtype):
            return sb.tile(shape, dtype, name=name, align_bytes=64)

        def bank(b, name, shape):
            return ps.tile(shape, F32, name=name, tag="bank%d" % b)

        def load_list(name, src):
            t = sb.tile([P, 32], U16, name=name)
            nc.sync.dma_start(t[:], src)
            return t

        def cleared(name, cols):
            t = sb.tile([P, cols], U8, name=name, tag=name, align_bytes=64)
            nc.vector.memset(t[:].bitcast(I32), 0)
            return t

        def load_scale_rows(dst, src, queues):
            for q in range(4):
                queues[q].dma_start(dst[QUAD * q : QUAD * q + 4, :].bitcast(I32), src[0, 4 * q : 4 * q + 4, :].bitcast(I32))

        def load_words(name, src, cols):
            t = tile(name, [P, cols], U32)
            nc.sync.dma_start(t[:].bitcast(I32), src[0].rearrange("p c r -> p (c r)").bitcast(I32))
            return t

        def load_fp4(name, src, queue):
            t = sb.tile([P, 2 * H], U8, name=name, tag=name, align_bytes=64)
            queue.dma_start(t[:].bitcast(I32), src[0].bitcast(I32))
            return t

        def deal_fp4(name, raw):
            t = tile(name, [P, 2 * H], U8)
            nc.vector.tensor_copy(
                t[:].bitcast(I32).rearrange("p (t g c) -> p t g c", t=PACK, c=4),
                raw[:].bitcast(I32).rearrange("p (g t c) -> p t g c", t=PACK, c=4),
            )
            return t

        def deal_scales(name, raw):
            t = tile(name, [P, H], U8)
            nc.vector.tensor_copy(
                t[:].bitcast(I32).rearrange("p (t g c) -> p t g c", t=PACK, c=2),
                raw[:].bitcast(I32).rearrange("p (g t c) -> p t g c", t=PACK, c=2),
            )
            return t

        def halves(offsets):
            return [(slice(h * HALF, (h + 1) * HALF), offsets[:, 16 * h : 16 * (h + 1)]) for h in range(2)]

        def load_unit(name, queue, src):
            t = tile(name, [P, P], F32)
            nc.gpsimd.memset(t[:], 0.0)
            queue.dma_start(
                t[0:PACK, :].rearrange("t (g r) -> t g r", r=8),
                src.rearrange("(g t r) o -> t g (r o)", t=PACK, r=8),
            )
            return t

        ws2_raw = cleared("ws2_raw", H)
        es_all = cleared("es_all", W)
        ws3_raw = cleared("ws3_raw", H)
        ws1_raw = cleared("ws1_raw", H)
        unit_rows = load_unit("unit_rows", nc.gpsimd, unit)
        ident = tile("ident", [P, P], F32)
        make_identity(nc, ident[:])

        offs_t = load_list("offs_t", offs)
        vol_col = tile("vol_col", [P, 8], F32)
        nc.scalar.dma_start(vol_col[:], vol[0].rearrange("(p c) -> p c", c=8))
        xs_all = tile("xs_all", [P, T], U8)
        for q, queue in enumerate((nc.sync, nc.sync, nc.scalar, nc.scalar)):
            rows4 = x_scales[0, 4 * q : 4 * q + 4, :].bitcast(I32)
            queue.dma_start(xs_all[QUAD * q : QUAD * (q + 1), :].bitcast(I32), rows4.partition_broadcast(8))
        xw_all = load_words("xw_all", x_words, T)
        w2_raw = load_fp4("w2_raw", w2_words, nc.scalar)
        hdg_t = load_list("hdg_t", hdg)
        load_scale_rows(ws2_raw[:], w2_scales, (nc.sync,) * 4)
        ew_all = load_words("ew_all", e_words, W)
        load_scale_rows(es_all[:], e_scales, (nc.sync,) * 4)
        unit2_rows = load_unit("unit2_rows", nc.sync, unit2)
        w3_raw = load_fp4("w3_raw", w3_words, nc.sync)
        load_scale_rows(ws3_raw[:], w3_scales, (nc.sync,) * 4)
        sec_t = load_list("sec_t", sec)
        load_scale_rows(ws1_raw[:], w1_scales, (nc.sync,) * 4)
        w1_raw = load_fp4("w1_raw", w1_words, nc.sync)
        prx_t = load_list("prx_t", prx)

        inv_col = tile("inv_col", [P, 8], F32)
        nc.vector.reciprocal(inv_col[:], vol_col[:])
        xs = tile("xs", [P, S], U8)
        nc.vector.tensor_copy(xs[:], xs_all[:].indirect(offs_t[:]))

        inv_all = tile("inv_all", [P, P, 8], F32)
        for b in range(2):
            spread = bank(5 + b, "spread%d" % b, [P, 4, P])
            for c in range(4):
                col = 4 * b + c
                nc.tensor.transpose(spread[:, c, :], inv_col[:, col : col + 1].to_broadcast([P, P]), ident[:])
            nc.scalar.activation(inv_all[:, :, 4 * b : 4 * b + 4], spread[:].rearrange("p c n -> p n c"), ACT.Copy)
        turned = bank(7, "turned", [P, P])
        nc.tensor.transpose(turned[:], unit_rows[:], ident[:])
        unit_col = tile("unit_col", [P, PACK], F32)
        half_unit = tile("half_unit", [P, PACK], F32)
        nc.scalar.activation(half_unit[:], turned[:, 0:PACK], ACT.Copy, scale=0.5)
        nc.scalar.activation(unit_col[:], turned[:, 0:PACK], ACT.Copy)
        inv_vol = tile("inv_vol", [P, Z], F32)
        nc.scalar.activation(inv_vol[:], inv_all[:].rearrange("p n c -> p (n c)").indirect(hdg_t[:]), ACT.Copy)

        w2 = deal_fp4("w2", w2_raw)
        xw = tile("xw", [P, S], U32)
        nc.vector.tensor_copy(xw[:], xw_all[:].indirect(offs_t[:]))
        ws2 = deal_scales("ws2", ws2_raw)

        def product(out, w, w_scales, t, words, scales):
            nc.tensor.matmul_mx(
                out,
                lhsT=w[:, 2 * P * t : 2 * P * (t + 1)].bitcast(FP4X4),
                lhsT_scale=w_scales[:, P * t : P * (t + 1)],
                rhs=words.bitcast(FP8X4),
                rhs_scale=scales,
                start=True,
                stop=True,
            )

        yv_ps = [bank(t, "yv%d" % t, [P, S]) for t in range(PACK)]
        for t in range(PACK):
            product(yv_ps[t][:], w2, ws2, t, xw[:], xs[:])

        ew = tile("ew", [P, Z], U32)
        nc.vector.tensor_copy(ew[:], ew_all[:].indirect(hdg_t[:]))
        es_front = tile("es_front", [P, HALF], U8)
        nc.vector.tensor_copy(es_front[:], es_all[:].indirect(hdg_t[:, 0:16]))
        turned2 = bank(7, "turned2", [P, P])
        nc.tensor.transpose(turned2[:], unit2_rows[:], ident[:])
        unit2_col = tile("unit2_col", [P, PACK], F32)
        nc.vector.tensor_copy(unit2_col[:], turned2[:, 0:PACK])
        w3 = deal_fp4("w3", w3_raw)
        ws3 = deal_scales("ws3", ws3_raw)
        es_back = sb.tile([P, HALF], U8, name="es_back", tag="ws3_raw", align_bytes=64)
        nc.vector.tensor_copy(es_back[:], es_all[:].indirect(hdg_t[:, 16:32]))
        ws1 = deal_scales("ws1", ws1_raw)
        w1 = deal_fp4("w1", w1_raw)

        yv = [tile("yv_sb%d" % t, [P, S], F32) for t in range(PACK)]
        vs = [sb.tile([P, S], F32, name="vs%d" % t, tag="vs%d" % t, align_bytes=64) for t in range(PACK)]

        def empty_yv(t):
            nc.scalar.activation(yv[t][:], yv_ps[t][:], ACT.Copy, scale=half_unit[:, t : t + 1])

        def fetch_vs(t):
            for cols, offsets in halves(sec_t):
                nc.scalar.activation(vs[t][:, cols], yv[t][:].indirect(offsets), ACT.Copy)

        for t in range(PACK):
            empty_yv(t)
        for t in range(PACK):
            fetch_vs(t)

        front_bf = tile("front_bf", [P, 2 * P, PACK], BF16)
        third_bf = sb.tile([P, P, PACK], BF16, name="third_bf", tag="w1_raw", align_bytes=64)
        last_bf = tile("last_bf", [P, P, PACK], BF16)
        ye_ps = [bank(c, "ye%d" % c, [P, PACK, P]) for c in range(4)]
        for c in range(4):
            cols = slice(P * c, P * (c + 1))
            es = (es_front, es_back)[c // 2][:, P * (c % 2) : P * (c % 2 + 1)]
            for t in range(PACK):
                product(ye_ps[c][:, t, :], w3, ws3, t, ew[:, cols], es)
            if c < 3:
                nc.vector.tensor_tensor(
                    front_bf[:, cols, :] if c < 2 else third_bf[:],
                    ye_ps[c][:].rearrange("p t n -> p n t"),
                    unit2_col[:].unsqueeze(1).to_broadcast([P, P, PACK]),
                    ALU.mult,
                )

        y_ps = [bank(4 + t, "y%d" % t, [P, S]) for t in range(PACK)]
        for t in range(PACK):
            product(y_ps[t][:], w1, ws1, t, xw[:], xs[:])

        planes = tile("planes", [P, PACK, S], BF16)

        def combine(t):
            nc.vector.scalar_tensor_tensor(
                planes[:, t, :],
                y_ps[t][:],
                unit_col[:, t : t + 1],
                vs[t][:],
                ALU.mult,
                ALU.add,
            )

        hid2_w = tile("hid2_w", [P, Z], U32)
        hid2_s = tile("hid2_s", [P, Z], U8)

        def quantise2(cols, src):
            nc.vector.quantize_mx(hid2_w[:, cols].bitcast(FP8X4), hid2_s[:, cols], src[:].rearrange("p c t -> p (c t)"))

        quantise2(slice(0, 2 * P), front_bf)
        combine(0)
        last_planes = sb.tile([P, PACK, P], BF16, name="last_planes", tag="vs0", align_bytes=64)
        for t in range(PACK):
            nc.scalar.activation(last_planes[:, t, :], ye_ps[3][:, t, :], ACT.Copy, scale=unit2_col[:, t : t + 1])
        nc.scalar.copy(
            last_bf[:].rearrange("p (c i) t -> p c t i", i=4),
            last_planes[:].rearrange("p t (c i) -> p c t i", i=4),
        )
        quantise2(slice(2 * P, 3 * P), third_bf)
        for t in range(1, PACK):
            combine(t)
        quantise2(slice(3 * P, 4 * P), last_bf)

        hid_bf = tile("hid_bf", [P, PACK, P, PACK], BF16)
        hid_w = [tile("hid_w%d" % r, [P, P], U32) for r in range(PACK)]
        hid_s = [tile("hid_s%d" % r, [P, P], U8) for r in range(PACK)]
        for pairs, copy in ((slice(0, WEAVE), nc.vector.tensor_copy), (slice(WEAVE, P // 2), nc.scalar.copy)):
            copy(
                hid_bf[:].rearrange("p r (a b) t -> p a r b t", b=2)[:, pairs],
                planes[:].rearrange("p t (a b r) -> p a r b t", b=2, r=PACK)[:, pairs],
            )
        for r in range(PACK):
            nc.vector.quantize_mx(hid_w[r][:].bitcast(FP8X4), hid_s[r][:], hid_bf[:, r].rearrange("p c t -> p (c t)"))

        sc_ps = [bank(r, "sc%d" % r, [P, Z]) for r in range(PACK)]
        for r in range(PACK):
            nc.tensor.matmul_mx(
                sc_ps[r][:], lhsT=hid_w[r][:].bitcast(FP8X4), lhsT_scale=hid_s[r][:],
                rhs=hid2_w[:].bitcast(FP8X4), rhs_scale=hid2_s[:], start=True, stop=True,
            )

        beta = [tile("beta%d" % r, [P, Z], F32) for r in range(PACK)]
        other = [tile("other%d" % r, [P, Z], F32) for r in range(PACK)]
        prod = [tile("prod%d" % r, [P, Z], F32) for r in range(PACK)]
        expl = [tile("expl%d" % r, [P, 1], F32) for r in range(PACK)]
        neg_expl = tile("neg_expl", [P, 1], F32)
        squares = tile("squares", [P, Z], BF16)
        res = tile("res", [P, PACK, Z], F32)
        out_rows = out_0.rearrange("(p r) e -> p r e", r=PACK)
        by_vector, by_scalar = (0, 1), (2, 3)

        for r in range(PACK):
            nc.vector.tensor_tensor(beta[r][:], sc_ps[r][:], inv_vol[:], ALU.mult)
        for r in by_vector:
            nc.gpsimd.tensor_scalar(other[r][:], beta[r][:], 1.0, 0.0, ALU.mult, ALU.add)

        def mean_square(r):
            nc.scalar.activation(squares[:], beta[r][:], ACT.Square, scale=Z ** -0.5, accum_out=expl[r][:])

        mean_square(0)
        nc.scalar.activation(neg_expl[:], expl[0][:], ACT.Copy, scale=-1.0)
        mean_square(1)
        for r in by_scalar:
            for cols, offsets in halves(prx_t):
                nc.scalar.activation(other[r][:, cols], beta[r][:].indirect(offsets), ACT.Copy)
        for r in by_scalar:
            mean_square(r)
        for r in by_vector:
            for cols, offsets in halves(prx_t):
                nc.vector.tensor_tensor(prod[r][:, cols], beta[r][:].indirect(offsets), other[r][:, cols], ALU.mult)
        for r in by_scalar:
            nc.vector.tensor_tensor(prod[r][:], other[r][:], beta[r][:], ALU.mult)
        nc.scalar.activation(res[:, 0, :], prod[0][:], ACT.Identity, bias=neg_expl[:])
        nc.sync.dma_start(out_rows[:, 0, :], res[:, 0, :])
        for r in range(1, PACK):
            nc.vector.tensor_scalar(res[:, r, :], prod[r][:], expl[r][:], None, ALU.subtract)
            nc.sync.dma_start(out_rows[:, r, :], res[:, r, :])

        res_bf = tile("res_bf", [P, Z, PACK], BF16)
        shares = (
            (slice(0, HALF), nc.vector.tensor_copy),
            (slice(HALF, SPLIT), nc.vector.tensor_copy),
            (slice(SPLIT, Z), nc.scalar.copy),
        )
        for cols, copy in shares:
            copy(
                res_bf[:, cols, :].rearrange("p (c i) r -> p c r i", i=4),
                res[:, :, cols].rearrange("p r (c i) -> p c r i", i=4),
            )
        res_w = tile("res_w", [P, Z], U32)
        res_s = tile("res_s", [P, Z], U8)
        out_words = out_1[0].rearrange("p c r -> p (c r)").bitcast(I32)
        for h in range(2):
            cols = slice(h * HALF, (h + 1) * HALF)
            nc.vector.quantize_mx(res_w[:, cols].bitcast(FP8X4), res_s[:, cols], res_bf[:, cols, :].rearrange("p c r -> p (c r)"))
            nc.sync.dma_start(out_words[:, cols], res_w[:, cols].bitcast(I32))
        for q in range(4):
            (nc.scalar, nc.sync)[q % 2].dma_start(out_2[0, 4 * q : 4 * q + 4, :].bitcast(I32), res_s[QUAD * q : QUAD * q + 4, :].bitcast(I32))
